import numpy as np
import ml_dtypes


def mxq(x, axis, fmt="e4m3"):
    dtype, down = {"e4m3": (ml_dtypes.float8_e4m3fn, 7), "e5m2": (ml_dtypes.float8_e5m2, 14)}[fmt]
    v = np.moveaxis(np.asarray(x, np.float32).astype(ml_dtypes.bfloat16).astype(np.float64), axis, -1)
    blocks = v.reshape(v.shape[:-1] + (-1, 32))
    amax = np.abs(blocks).max(-1, keepdims=True)
    byte = np.maximum(np.where(amax > 0, np.frexp(amax)[1] - 1 + 127, 0) - down, 1)
    scale = np.exp2(byte - 127.0)
    codes = (blocks / scale).astype(np.float32).astype(dtype).astype(np.float64)
    return np.moveaxis((codes * scale).reshape(v.shape), -1, axis)


WIDE = False


def mx_kscale(k):
    if not WIDE:
        return np.ones(k)
    levels = np.array([10, -10, 5, -5, 0])
    if k % 512:
        return np.exp2(np.random.permutation(np.resize(levels, k // 32))).repeat(32)
    a = np.empty((k // 512, 16))
    for p in range(k // 512):
        a[p, :8] = np.random.permutation(np.resize(levels, 8))
        for g in range(8):
            far = levels[np.abs(levels - a[p, g]) >= 10]
            a[p, g + 8] = far[np.random.randint(len(far))]
    return np.exp2(a.ravel()).repeat(32)


BF16 = ml_dtypes.bfloat16


def bf(x):
    return np.asarray(x, np.float32).astype(BF16)


def f64(x):
    return np.asarray(x).astype(np.float64)


E2M1 = np.array([0.0, 0.5, 1.0, 1.5, 2.0, 3.0, 4.0, 6.0, -0.0, -0.5, -1.0, -1.5, -2.0, -3.0, -4.0, -6.0])


def pack_weight(w, fmt):
    k, n = w.shape
    w = f64(bf(w)).reshape(k // 32, 32, n)
    amax = np.abs(w).max(1)
    if fmt == "e4m3":
        byte = np.frexp(amax)[1] - 1 + 127 - 7
    else:
        mant, ex = np.frexp(amax / 6.0)
        byte = np.where(mant > 0.5, ex, ex - 1) + 127
    byte = np.clip(np.where(amax > 0, byte, 1), 1, 254)
    scaled = (w * np.exp2(127.0 - byte)[:, None, :]).reshape(k, n).astype(np.float32)
    by_word = np.ascontiguousarray(scaled.reshape(k // 512, 128, 4, n).transpose(0, 1, 3, 2))
    if fmt == "e4m3":
        words = by_word.astype(ml_dtypes.float8_e4m3fn).view(np.uint8)
    else:
        c = by_word.astype(ml_dtypes.float4_e2m1fn).view(np.uint8) & 0xF
        words = c[..., 0::2] | (c[..., 1::2] << 4)
    return np.ascontiguousarray(words), np.ascontiguousarray(byte.astype(np.uint8).reshape(k // 512, 16, n))


def unpack_weight(words, scales, fmt):
    g, p, n, _ = words.shape
    if fmt == "e4m3":
        vals = np.ascontiguousarray(words).view(ml_dtypes.float8_e4m3fn).astype(np.float64)
    else:
        nib = np.empty((g, p, n, 4), np.uint8)
        nib[..., 0::2] = words & 0xF
        nib[..., 1::2] = words >> 4
        vals = E2M1[nib]
    vals = vals * np.repeat(np.exp2(scales.astype(np.float64) - 127.0), 8, axis=1)[..., None]
    return vals.transpose(0, 1, 3, 2).reshape(g * 512, n)
def pack4(w):
    words, scales = pack_weight(w, "e2m1")
    return words.reshape(words.shape[0], 128, -1), scales


def unpack4(words, scales):
    return unpack_weight(words.reshape(words.shape[0], 128, -1, 2), scales, "e2m1")


def planes(Y):
    n, m = Y.shape
    b = f64(bf(Y)).reshape(n // 32, 32, m)
    amax = np.abs(b).max(1)
    byte = np.clip(np.where(amax > 0, np.frexp(amax)[1] - 1 + 127 - 7, 1), 1, 254)
    codes = (b * np.exp2(127.0 - byte)[:, None, :]).reshape(n, m).astype(np.float32).astype(ml_dtypes.float8_e4m3fn).view(np.uint8)
    words = codes.reshape(n // 512, 128, 4, m).transpose(0, 1, 3, 2)
    return np.ascontiguousarray(words), np.ascontiguousarray(byte.astype(np.uint8).reshape(n // 512, 16, m))


L, N, P, D = 4, 1024, 512, 512


def softplus(s):
    return np.maximum(s, 0.0) + np.log(1.0 + np.exp(-np.abs(s)))


def setup_inputs():
    p, q = mx_kscale(D), mx_kscale(D)
    a = bf(np.random.standard_normal((N, D)) * p[None, :])
    u = bf(np.random.standard_normal((L, D)))
    r_words, r_scales = pack4(np.random.standard_normal((D, D)) / np.sqrt(D) / p[:, None])
    v = bf(np.random.standard_normal((L, D)) * q[None, :])
    b_words, b_scales = pack4((np.random.standard_normal((P, D)) * 2.0 / np.sqrt(D) / q[None, :]).T)
    return {
        "a": a,
        "u": u,
        "r_words": r_words,
        "r_scales": r_scales,
        "v": v,
        "b_words": b_words,
        "b_scales": b_scales,
        "x": bf(np.random.uniform(0.0, 1.0, (L, N, P))),
    }


def core(a, u, r_words, r_scales, v, b_words, b_scales, x):
    au = f64(a)[None, :, :] * f64(u)[:, None, :]
    t = mxq(au, 2, "e4m3") @ unpack4(r_words, r_scales)
    tv = t * f64(v)[:, None, :]
    s = mxq(tv, 2, "e4m3") @ unpack4(b_words, b_scales)
    return softplus(s) - f64(x) * s


def reference(a, u, r_words, r_scales, v, b_words, b_scales, x):
    R_out = core(a, u, r_words, r_scales, v, b_words, b_scales, x)
    words, scales = planes(np.moveaxis(R_out, 2, 0).reshape(512, -1))
    return R_out, words, scales

@@ -1,0 +1,336 @@
+from contextlib import ExitStack
+
+import concourse.mybir as mybir
+from concourse.masks import make_identity
+
+L, N, D, P = 4, 1024, 512, 512
+FLOPS = 2 * L * N * D * D + 2 * L * N * D * P
+
+F32 = mybir.dt.float32
+BF16 = mybir.dt.bfloat16
+I32 = mybir.dt.int32
+U32 = mybir.dt.uint32
+U8 = mybir.dt.uint8
+FP8 = mybir.dt.float8_e4m3fn_x4
+FP4 = mybir.dt.float4_e2m1fn_x4
+ALU = mybir.AluOpType
+ACTF = mybir.ActivationFunctionType
+
+TILES = N // 128
+PAIRS = TILES // 2
+DELTA = 2.0 ** -63
+
+
+def tile_dualdomaindedicomlogisticloss_x2_kernel(
+    tc, a, u, r_words, r_scales, v, b_words, b_scales, x, out_0, out_1, out_2
+):
+    nc = tc.nc
+    words_out = out_1[0].rearrange("p m t -> p (m t)")
+
+    with ExitStack() as ctx:
+        keep = ctx.enter_context(tc.tile_pool(name="keep", bufs=1))
+        work = ctx.enter_context(tc.tile_pool(name="work", bufs=2))
+        psum = ctx.enter_context(tc.psum_pool(name="psum", bufs=2))
+        ctx.enter_context(tc.manual_schedule())
+
+        rs_raw = keep.tile([128, D], U8, name="rs_raw", align_bytes=64)
+        bs = keep.tile([128, P], U8, name="bs", align_bytes=64)
+        nc.vector.memset(rs_raw[:].bitcast(I32), 0)
+        nc.vector.memset(bs[:].bitcast(I32), 0)
+        ident = keep.tile([128, 128], F32, name="ident")
+        make_identity(nc, ident[:])
+
+        a_sb = []
+        for j in range(PAIRS):
+            a_j = keep.tile([128, 2, D], BF16, name="a%d" % j)
+            nc.sync.dma_start(out=a_j[:], in_=a[256 * j : 256 * j + 256, :].rearrange("(i p) k -> p i k", p=128))
+            a_sb.append(a_j)
+        rw_raw = keep.tile([128, 2 * D], U8, name="rw_raw", align_bytes=64)
+        bw = keep.tile([128, 2 * P], U8, name="bw", align_bytes=64)
+        u_sb = keep.tile([128, L, 4], BF16, name="u_sb")
+        v_sb = keep.tile([128, L, 4], BF16, name="v_sb")
+        nc.scalar.dma_start(out=rw_raw[:].bitcast(I32), in_=r_words[0].bitcast(I32))
+        nc.scalar.dma_start(out=u_sb[:], in_=u.rearrange("l (p t) -> p l t", t=4))
+        nc.scalar.dma_start(out=v_sb[:], in_=v.rearrange("l (p t) -> p l t", t=4))
+        for q in range(4):
+            nc.scalar.dma_start(
+                out=rs_raw[32 * q : 32 * q + 4, :].bitcast(I32), in_=r_scales[0, 4 * q : 4 * q + 4, :].bitcast(I32)
+            )
+        nc.sync.dma_start(out=bw[:].bitcast(I32), in_=b_words[0].bitcast(I32))
+        for q in range(4):
+            nc.sync.dma_start(
+                out=bs[32 * q : 32 * q + 4, :].bitcast(I32), in_=b_scales[0, 4 * q : 4 * q + 4, :].bitcast(I32)
+            )
+        x_sb = []
+        for l in range(L):
+            x_l = keep.tile([128, TILES, P], BF16, name="x%d" % l)
+            nc.sync.dma_start(out=x_l[:], in_=x[l].rearrange("(i p) k -> p i k", p=128))
+            x_sb.append(x_l)
+
+        rw = keep.tile([128, 4, 256], U8, name="rw", align_bytes=64)
+        rs = keep.tile([128, 4, 128], U8, name="rs", align_bytes=64)
+
+        def permute_r():
+            nc.vector.tensor_copy(
+                out=rw[:].rearrange("p t (m b) -> p t m b", b=2),
+                in_=rw_raw[:].rearrange("p (m t b) -> p t m b", t=4, b=2),
+            )
+            nc.vector.tensor_copy(out=rs[:], in_=rs_raw[:].rearrange("p (m t) -> p t m", t=4))
+
+        aT = []
+        for h in range(2):
+            aT_h = keep.tile([128, 512, 4], BF16, name="aT%d" % h, align_bytes=64)
+            aT.append(aT_h)
+
+        def transpose_a(j):
+            ps = psum.tile([128, 2, 2, 128], F32, name="ps_a", tag="o")
+            words = a_sb[j][:].bitcast(F32)
+            for i in range(2):
+                for k in range(2):
+                    nc.tensor.transpose(ps[:, i, k, :], words[:, i, k : 256 : 2], ident[:])
+            c0 = 256 * (j % 2)
+            dst = aT[j // 2][:, c0 : c0 + 256, :].bitcast(F32).rearrange("p (i n) k -> p i n k", i=2)
+            src = ps[:].rearrange("p i k n -> p i n k")
+            if j % 2 == 0:
+                nc.scalar.copy(out=dst, in_=src)
+            else:
+                nc.vector.tensor_copy(out=dst, in_=src)
+
+        st = {}
+
+        def scale_a(l, h):
+            auq = work.tile([128, 512, 4], BF16, name="auq", bufs=2, align_bytes=64)
+            nc.vector.tensor_tensor(
+                out=auq[:], in0=aT[h][:], in1=u_sb[:, l, :].unsqueeze(1).to_broadcast([128, 512, 4]), op=ALU.mult
+            )
+            st["auq", l, h] = auq
+
+        def quant_a(l, h):
+            c = work.tile([128, 512], U32, name="au_c", bufs=2, align_bytes=64)
+            s = work.tile([128, 512], U8, name="au_s", bufs=2, align_bytes=64)
+            nc.vector.quantize_mx(
+                out=c[:].bitcast(FP8), scales=s[:], in_=st["auq", l, h][:].rearrange("p n t -> p (n t)")
+            )
+            st["au", l, h] = (c, s)
+
+        def matmul_1(l, i):
+            c, s = st["au", l, i // 4]
+            n0 = 128 * (i % 4)
+            ps = psum.tile([128, 4, 128], F32, name="ps_t", tag="t")
+            for t in range(4):
+                nc.tensor.matmul_mx(
+                    out=ps[:, t, :],
+                    lhsT=rw[:, t, :].bitcast(FP4),
+                    lhsT_scale=rs[:, t, :],
+                    rhs=c[:, n0 : n0 + 128].bitcast(FP8),
+                    rhs_scale=s[:, n0 : n0 + 128],
+                    start=True,
+                    stop=True,
+                )
+            st["t", l, i] = ps
+
+        def scale_t(l, i):
+            if i % 2 == 0:
+                tvq = work.tile([128, 256, 4], BF16, name="tvq", bufs=3, align_bytes=64)
+                st["tvq", l, i // 2] = tvq
+            tvq = st["tvq", l, i // 2]
+            n0 = 128 * (i % 2)
+            nc.vector.tensor_tensor(
+                out=tvq[:, n0 : n0 + 128, :],
+                in0=st["t", l, i][:].rearrange("p t n -> p n t"),
+                in1=v_sb[:, l, :].unsqueeze(1).to_broadcast([128, 128, 4]),
+                op=ALU.mult,
+            )
+
+        def quant_t(l, j):
+            c = work.tile([128, 256], U32, name="tv_c", bufs=8, align_bytes=64)
+            s = work.tile([128, 256], U8, name="tv_s", bufs=8, align_bytes=64)
+            nc.vector.quantize_mx(
+                out=c[:].bitcast(FP8), scales=s[:], in_=st["tvq", l, j][:].rearrange("p n t -> p (n t)")
+            )
+            st["tv", l, j] = (c, s)
+
+        def matmul_2(l, i, tag):
+            c, s = st["tv", l, i // 2]
+            n0 = 128 * (i % 2)
+            ps = psum.tile([128, P], F32, name="ps_" + tag, tag=tag)
+            nc.tensor.matmul_mx(
+                out=ps[:],
+                lhsT=c[:, n0 : n0 + 128].bitcast(FP8),
+                lhsT_scale=s[:, n0 : n0 + 128],
+                rhs=bw[:].bitcast(FP4),
+                rhs_scale=bs[:],
+                start=True,
+                stop=True,
+            )
+            return ps
+
+        def sigmoid(l, i):
+            ps = matmul_2(l, i, "s1")
+            if i % 2 == 0:
+                sg = work.tile([128, 2, P], F32, name="sg", bufs=8)
+                st["sg", l, i // 2] = sg
+            nc.scalar.activation(out=st["sg", l, i // 2][:, i % 2, :], in_=ps[:], func=ACTF.Sigmoid, scale=-1.0)
+
+        def log(l, j):
+            sg = st["sg", l, j]
+            nc.scalar.activation(out=sg[:], in_=sg[:], func=ACTF.Ln, bias=DELTA)
+
+        def scores(l, i):
+            st["s", l, i] = matmul_2(l, i, "s2")
+
+        def loss_parts(l, i):
+            ps = st["s", l, i]
+            xs = work.tile([128, P], F32, name="xs", bufs=4)
+            nc.vector.tensor_tensor(out=xs[:], in0=ps[:], in1=x_sb[l][:, i, :], op=ALU.mult)
+            sp = work.tile([128, P], F32, name="sp", bufs=4)
+            nc.vector.scalar_tensor_tensor(
+                out=sp[:], in0=st["sg", l, i // 2][:, i % 2, :], scalar=-1.0, in1=ps[:], op0=ALU.mult, op1=ALU.max
+            )
+            st["parts", l, i] = (sp, xs)
+
+        def loss(l, i):
+            sp, xs = st["parts", l, i]
+            if i % 2 == 0:
+                res = work.tile([128, 2, P], F32, name="res", bufs=4)
+                st["res", l, i // 2] = res
+            res = st["res", l, i // 2]
+            engine = GP_ENGINE(nc, l, i)
+            for k in range(2):
+                cols = slice(256 * k, 256 * k + 256)
+                engine.tensor_tensor(out=res[:, i % 2, cols], in0=sp[:, cols], in1=xs[:, cols], op=ALU.subtract)
+            if i % 2 == 1:
+                n0 = 128 * (i - 1)
+                nc.sync.dma_start(
+                    out=out_0[l, n0 : n0 + 256, :].rearrange("(i p) k -> p i k", p=128), in_=res[:]
+                )
+
+        def transpose_out(l, i):
+            if i % 2 == 0:
+                oq = work.tile([128, 256, 4], BF16, name="oq", bufs=3, align_bytes=64)
+                st["oq", l, i // 2] = oq
+            oq = st["oq", l, i // 2]
+            res = st["res", l, i // 2]
+            ps = psum.tile([128, 4, 128], F32, name="ps_o", tag="o")
+            for t in range(4):
+                nc.tensor.transpose(ps[:, t, :], res[:, i % 2, t : P : 4], ident[:])
+            n0 = 128 * (i % 2)
+            nc.scalar.copy(out=oq[:, n0 : n0 + 128, :], in_=ps[:].rearrange("p t n -> p n t"))
+
+        def quant_out(l, j):
+            if j == 0:
+                o_s = work.tile([128, N], U8, name="o_s", bufs=2, align_bytes=64)
+                st["o_s", l] = o_s
+            if j % 2 == 0:
+                o_c = work.tile([128, 512], U32, name="o_c", bufs=2, align_bytes=64)
+                st["o_c", l, j // 2] = o_c
+            o_s = st["o_s", l]
+            o_c = st["o_c", l, j // 2]
+            c0 = 256 * (j % 2)
+            nc.vector.quantize_mx(
+                out=o_c[:, c0 : c0 + 256].bitcast(FP8),
+                scales=o_s[:, 256 * j : 256 * j + 256],
+                in_=st["oq", l, j][:].rearrange("p n t -> p (n t)"),
+            )
+            if j % 2 == 1:
+                m0 = N * l + 512 * (j // 2)
+                nc.sync.dma_start(out=words_out[:, 4 * m0 : 4 * m0 + 2048].bitcast(I32), in_=o_c[:].bitcast(I32))
+            if j == PAIRS - 1:
+                for q in range(4):
+                    nc.sync.dma_start(
+                        out=out_2[0, 4 * q : 4 * q + 4, N * l : N * l + N].bitcast(I32),
+                        in_=o_s[32 * q : 32 * q + 4, :].bitcast(I32),
+                    )
+
+        LAG = 4
+        pending = []
+        quants = []
+
+        def feed_transpose():
+            if pending:
+                l, i = pending.pop(0)
+                transpose_out(l, i)
+                if i % 2 == 1:
+                    quants.append((l, i // 2))
+
+        def feed_quant(keep_back):
+            if len(quants) > keep_back:
+                quant_out(*quants.pop(0))
+
+        def front(l, part):
+            if part == 0:
+                scale_a(l, 0)
+            elif part == 1:
+                scale_a(l, 1)
+            elif part == 2:
+                quant_a(l, 0)
+                matmul_1(l, 0)
+                matmul_1(l, 1)
+            elif part == 3:
+                quant_a(l, 1)
+
+        def slot_a(l, prev):
+            for i in range(TILES):
+                scale_t(l, i)
+                if i + 2 < TILES:
+                    matmul_1(l, i + 2)
+                if i % 2 == 0 and i > 0:
+                    quant_t(l, i // 2 - 1)
+                    sigmoid(l, i - 2)
+                    sigmoid(l, i - 1)
+                if i % 2 == 1:
+                    feed_transpose()
+                    feed_quant(1)
+                if i == 5 and prev >= 0:
+                    scores(prev, 0)
+                    scores(prev, 1)
+            quant_t(l, PAIRS - 1)
+            sigmoid(l, 6)
+            sigmoid(l, 7)
+
+        def slot_b(l):
+            for i in range(TILES):
+                loss_parts(l, i)
+                if i + 2 < TILES:
+                    scores(l, i + 2)
+                if l + 1 < L and i < PAIRS:
+                    log(l + 1, i)
+                loss(l, i)
+                if i >= LAG or l + 1 == L:
+                    feed_transpose()
+                if l + 1 == L and i >= 4 and len(pending) > 2:
+                    feed_transpose()
+                pending.append((l, i))
+                if i % 2 == 1:
+                    feed_quant(1)
+                if l + 2 < L and i >= 4:
+                    front(l + 2, i - 4)
+
+        transpose_a(0)
+        transpose_a(1)
+        permute_r()
+        front(0, 0)
+        front(0, 2)
+        transpose_a(2)
+        transpose_a(3)
+        front(0, 1)
+        front(0, 3)
+        slot_a(0, -1)
+        for j in range(PAIRS):
+            log(0, j)
+        for part in range(4):
+            front(1, part)
+        for l in range(L):
+            if l + 1 < L:
+                slot_a(l + 1, l)
+            else:
+                scores(l, 0)
+                scores(l, 1)
+            slot_b(l)
+        while pending or quants:
+            feed_transpose()
+            feed_quant(0 if not pending else 1)
+
+
+def GP_ENGINE(nc, l, i):
+    return nc.gpsimd if not (l == L - 1 and i >= 6) else nc.vector

@@ -19,6 +19,10 @@ ACTF = mybir.ActivationFunctionType
 TILES = N // 128
 PAIRS = TILES // 2
 DELTA = 2.0 ** -63
+G_TILES = 6
+AU_ACT = (1, 2)
+C0, C1, C2 = 0, 2, 4
+R_LAG, T_LAG, Q_LAG = 3, 3, 4
 
 
 def tile_dualdomaindedicomlogisticloss_x2_kernel(
@@ -41,21 +45,25 @@ def tile_dualdomaindedicomlogisticloss_x2_kernel(
         make_identity(nc, ident[:])
 
         a_sb = []
+        rw_raw = keep.tile([128, 2 * D], U8, name="rw_raw", align_bytes=64)
         for j in range(PAIRS):
             a_j = keep.tile([128, 2, D], BF16, name="a%d" % j)
             nc.sync.dma_start(out=a_j[:], in_=a[256 * j : 256 * j + 256, :].rearrange("(i p) k -> p i k", p=128))
             a_sb.append(a_j)
-        rw_raw = keep.tile([128, 2 * D], U8, name="rw_raw", align_bytes=64)
+            if j == 0:
+                nc.sync.dma_start(out=rw_raw[:].bitcast(I32), in_=r_words[0].bitcast(I32))
         bw = keep.tile([128, 2 * P], U8, name="bw", align_bytes=64)
         u_sb = keep.tile([128, L, 4], BF16, name="u_sb")
         v_sb = keep.tile([128, L, 4], BF16, name="v_sb")
-        nc.scalar.dma_start(out=rw_raw[:].bitcast(I32), in_=r_words[0].bitcast(I32))
         nc.scalar.dma_start(out=u_sb[:], in_=u.rearrange("l (p t) -> p l t", t=4))
-        nc.scalar.dma_start(out=v_sb[:], in_=v.rearrange("l (p t) -> p l t", t=4))
         for q in range(4):
             nc.scalar.dma_start(
                 out=rs_raw[32 * q : 32 * q + 4, :].bitcast(I32), in_=r_scales[0, 4 * q : 4 * q + 4, :].bitcast(I32)
             )
+        nc.scalar.dma_start(out=v_sb[:], in_=v.rearrange("l (p t) -> p l t", t=4))
+        warm = keep.tile([128, 1], F32, name="warm")
+        nc.vector.memset(warm[:], 0.0)
+        nc.scalar.activation(out=warm[:], in_=warm[:], func=ACTF.Sigmoid)
         nc.sync.dma_start(out=bw[:].bitcast(I32), in_=b_words[0].bitcast(I32))
         for q in range(4):
             nc.sync.dma_start(
@@ -70,11 +78,13 @@ def tile_dualdomaindedicomlogisticloss_x2_kernel(
         rw = keep.tile([128, 4, 256], U8, name="rw", align_bytes=64)
         rs = keep.tile([128, 4, 128], U8, name="rs", align_bytes=64)
 
-        def permute_r():
+        def permute_r_words():
             nc.vector.tensor_copy(
                 out=rw[:].rearrange("p t (m b) -> p t m b", b=2),
                 in_=rw_raw[:].rearrange("p (m t b) -> p t m b", t=4, b=2),
             )
+
+        def permute_r_scales():
             nc.vector.tensor_copy(out=rs[:], in_=rs_raw[:].rearrange("p (m t) -> p t m", t=4))
 
         aT = []
@@ -91,27 +101,63 @@ def tile_dualdomaindedicomlogisticloss_x2_kernel(
             c0 = 256 * (j % 2)
             dst = aT[j // 2][:, c0 : c0 + 256, :].bitcast(F32).rearrange("p (i n) k -> p i n k", i=2)
             src = ps[:].rearrange("p i k n -> p i n k")
-            if j % 2 == 0:
-                nc.scalar.copy(out=dst, in_=src)
-            else:
-                nc.vector.tensor_copy(out=dst, in_=src)
+            nc.scalar.copy(out=dst, in_=src)
 
         st = {}
 
-        def scale_a(l, h):
-            auq = work.tile([128, 512, 4], BF16, name="auq", bufs=2, align_bytes=64)
+        def scale_a(l, h, c0=0, w=512):
+            if c0 == 0:
+                auq = work.tile([128, 512, 4], BF16, name="auq", bufs=4, align_bytes=64)
+                st["auq", l, h] = auq
+            cols = slice(c0, c0 + w)
             nc.vector.tensor_tensor(
-                out=auq[:], in0=aT[h][:], in1=u_sb[:, l, :].unsqueeze(1).to_broadcast([128, 512, 4]), op=ALU.mult
+                out=st["auq", l, h][:, cols, :],
+                in0=aT[h][:, cols, :],
+                in1=u_sb[:, l, :].unsqueeze(1).to_broadcast([128, w, 4]),
+                op=ALU.mult,
             )
-            st["auq", l, h] = auq
 
-        def quant_a(l, h):
-            c = work.tile([128, 512], U32, name="au_c", bufs=2, align_bytes=64)
-            s = work.tile([128, 512], U8, name="au_s", bufs=2, align_bytes=64)
+        def make_diagonals(l):
+            diag = keep.tile([128, 4, 128], BF16, name="diag%d" % l)
+            for t in range(4):
+                nc.gpsimd.tensor_scalar(
+                    out=diag[:, t, :],
+                    in0=ident[:],
+                    scalar1=u_sb[:, l, t : t + 1],
+                    scalar2=0.0,
+                    op0=ALU.mult,
+                    op1=ALU.add,
+                )
+            st["diag", l] = diag
+
+        def scale_a_chunk(l, c):
+            if c % 4 == 0:
+                auq = work.tile([128, 512, 4], BF16, name="auq", bufs=4, align_bytes=64)
+                st["auq", l, c // 4] = auq
+            n0 = 128 * (c % 4)
+            ps = psum.tile([128, 4, 128], F32, name="ps_u", tag="o" if c % 2 else "s2")
+            for t in range(4):
+                nc.tensor.matmul(
+                    ps[:, t, :],
+                    lhsT=st["diag", l][:, t, :],
+                    rhs=aT[c // 4][:, n0 : n0 + 128, t],
+                    start=True,
+                    stop=True,
+                )
+            nc.scalar.copy(out=st["auq", l, c // 4][:, n0 : n0 + 128, :], in_=ps[:].rearrange("p t n -> p n t"))
+
+        def quant_a(l, h, c0=0, w=512):
+            if c0 == 0:
+                c = work.tile([128, 512], U32, name="au_c", bufs=2, align_bytes=64)
+                s = work.tile([128, 512], U8, name="au_s", bufs=2, align_bytes=64)
+                st["au", l, h] = (c, s)
+            c, s = st["au", l, h]
+            cols = slice(c0, c0 + w)
             nc.vector.quantize_mx(
-                out=c[:].bitcast(FP8), scales=s[:], in_=st["auq", l, h][:].rearrange("p n t -> p (n t)")
+                out=c[:, cols].bitcast(FP8),
+                scales=s[:, cols],
+                in_=st["auq", l, h][:, cols, :].rearrange("p n t -> p (n t)"),
             )
-            st["au", l, h] = (c, s)
 
         def matmul_1(l, i):
             c, s = st["au", l, i // 4]
@@ -143,8 +189,8 @@ def tile_dualdomaindedicomlogisticloss_x2_kernel(
             )
 
         def quant_t(l, j):
-            c = work.tile([128, 256], U32, name="tv_c", bufs=8, align_bytes=64)
-            s = work.tile([128, 256], U8, name="tv_s", bufs=8, align_bytes=64)
+            c = work.tile([128, 256], U32, name="tv_c", bufs=12, align_bytes=64)
+            s = work.tile([128, 256], U8, name="tv_s", bufs=12, align_bytes=64)
             nc.vector.quantize_mx(
                 out=c[:].bitcast(FP8), scales=s[:], in_=st["tvq", l, j][:].rearrange("p n t -> p (n t)")
             )
@@ -168,7 +214,7 @@ def tile_dualdomaindedicomlogisticloss_x2_kernel(
         def sigmoid(l, i):
             ps = matmul_2(l, i, "s1")
             if i % 2 == 0:
-                sg = work.tile([128, 2, P], F32, name="sg", bufs=8)
+                sg = work.tile([128, 2, P], F32, name="sg", bufs=14)
                 st["sg", l, i // 2] = sg
             nc.scalar.activation(out=st["sg", l, i // 2][:, i % 2, :], in_=ps[:], func=ACTF.Sigmoid, scale=-1.0)
 
@@ -181,9 +227,9 @@ def tile_dualdomaindedicomlogisticloss_x2_kernel(
 
         def loss_parts(l, i):
             ps = st["s", l, i]
-            xs = work.tile([128, P], F32, name="xs", bufs=4)
+            xs = work.tile([128, P], F32, name="xs", bufs=5)
             nc.vector.tensor_tensor(out=xs[:], in0=ps[:], in1=x_sb[l][:, i, :], op=ALU.mult)
-            sp = work.tile([128, P], F32, name="sp", bufs=4)
+            sp = work.tile([128, P], F32, name="sp", bufs=5)
             nc.vector.scalar_tensor_tensor(
                 out=sp[:], in0=st["sg", l, i // 2][:, i % 2, :], scalar=-1.0, in1=ps[:], op0=ALU.mult, op1=ALU.max
             )
@@ -195,34 +241,37 @@ def tile_dualdomaindedicomlogisticloss_x2_kernel(
                 res = work.tile([128, 2, P], F32, name="res", bufs=4)
                 st["res", l, i // 2] = res
             res = st["res", l, i // 2]
-            engine = GP_ENGINE(nc, l, i)
-            for k in range(2):
-                cols = slice(256 * k, 256 * k + 256)
-                engine.tensor_tensor(out=res[:, i % 2, cols], in0=sp[:, cols], in1=xs[:, cols], op=ALU.subtract)
+            engine = nc.vector if i >= G_TILES else nc.gpsimd
+            engine.tensor_tensor(out=res[:, i % 2, :], in0=sp[:], in1=xs[:], op=ALU.subtract)
             if i % 2 == 1:
                 n0 = 128 * (i - 1)
                 nc.sync.dma_start(
                     out=out_0[l, n0 : n0 + 256, :].rearrange("(i p) k -> p i k", p=128), in_=res[:]
                 )
 
-        def transpose_out(l, i):
-            if i % 2 == 0:
-                oq = work.tile([128, 256, 4], BF16, name="oq", bufs=3, align_bytes=64)
-                st["oq", l, i // 2] = oq
-            oq = st["oq", l, i // 2]
-            res = st["res", l, i // 2]
-            ps = psum.tile([128, 4, 128], F32, name="ps_o", tag="o")
-            for t in range(4):
-                nc.tensor.transpose(ps[:, t, :], res[:, i % 2, t : P : 4], ident[:])
-            n0 = 128 * (i % 2)
-            nc.scalar.copy(out=oq[:, n0 : n0 + 128, :], in_=ps[:].rearrange("p t n -> p n t"))
+        def round_out(l, i):
+            rb = work.tile([128, P], BF16, name="rb", bufs=4)
+            nc.scalar.copy(out=rb[:], in_=st["res", l, i // 2][:, i % 2, :])
+            st["rb", l, i] = rb
+
+        def transpose_out(l, j):
+            oq = work.tile([128, 256, 4], BF16, name="oq", bufs=4, align_bytes=64)
+            ps = psum.tile([128, 2, 2, 128], F32, name="ps_o", tag="o")
+            for i in range(2):
+                words = st["rb", l, 2 * j + i][:].bitcast(F32)
+                for k in range(2):
+                    nc.tensor.transpose(ps[:, i, k, :], words[:, k : 256 : 2], ident[:])
+            nc.scalar.copy(
+                out=oq[:].bitcast(F32).rearrange("p (i n) k -> p i n k", i=2), in_=ps[:].rearrange("p i k n -> p i n k")
+            )
+            st["oq", l, j] = oq
 
         def quant_out(l, j):
             if j == 0:
                 o_s = work.tile([128, N], U8, name="o_s", bufs=2, align_bytes=64)
                 st["o_s", l] = o_s
             if j % 2 == 0:
-                o_c = work.tile([128, 512], U32, name="o_c", bufs=2, align_bytes=64)
+                o_c = work.tile([128, 512], U32, name="o_c", bufs=4, align_bytes=64)
                 st["o_c", l, j // 2] = o_c
             o_s = st["o_s", l]
             o_c = st["o_c", l, j // 2]
@@ -242,95 +291,164 @@ def tile_dualdomaindedicomlogisticloss_x2_kernel(
                         in_=o_s[32 * q : 32 * q + 4, :].bitcast(I32),
                     )
 
-        LAG = 4
-        pending = []
-        quants = []
+        clock = [0]
+        due = {}
 
-        def feed_transpose():
-            if pending:
-                l, i = pending.pop(0)
-                transpose_out(l, i)
-                if i % 2 == 1:
-                    quants.append((l, i // 2))
+        def later(steps, fn, *args):
+            due.setdefault(clock[0] + steps, []).append((fn, args))
 
-        def feed_quant(keep_back):
-            if len(quants) > keep_back:
-                quant_out(*quants.pop(0))
+        def tick():
+            for fn, args in due.pop(clock[0], []):
+                fn(*args)
+            clock[0] += 1
 
-        def front(l, part):
-            if part == 0:
+        def finish_tile(l, i):
+            round_out(l, i)
+            if i % 2 == 1:
+                later(T_LAG, finish_pair, l, i // 2)
+
+        def finish_pair(l, j):
+            transpose_out(l, j)
+            later(Q_LAG, quant_out, l, j)
+
+        def front(l):
+            if l not in AU_ACT:
                 scale_a(l, 0)
-            elif part == 1:
                 scale_a(l, 1)
-            elif part == 2:
-                quant_a(l, 0)
-                matmul_1(l, 0)
-                matmul_1(l, 1)
-            elif part == 3:
-                quant_a(l, 1)
+            quant_a(l, 0)
+            quant_a(l, 1)
 
-        def slot_a(l, prev):
+        def slot_a(l, acts):
             for i in range(TILES):
                 scale_t(l, i)
                 if i + 2 < TILES:
                     matmul_1(l, i + 2)
                 if i % 2 == 0 and i > 0:
                     quant_t(l, i // 2 - 1)
-                    sigmoid(l, i - 2)
-                    sigmoid(l, i - 1)
-                if i % 2 == 1:
-                    feed_transpose()
-                    feed_quant(1)
-                if i == 5 and prev >= 0:
-                    scores(prev, 0)
-                    scores(prev, 1)
+                acts(i)
+                tick()
             quant_t(l, PAIRS - 1)
-            sigmoid(l, 6)
-            sigmoid(l, 7)
 
-        def slot_b(l):
+        def slot_b(l, acts):
             for i in range(TILES):
                 loss_parts(l, i)
                 if i + 2 < TILES:
                     scores(l, i + 2)
-                if l + 1 < L and i < PAIRS:
-                    log(l + 1, i)
-                loss(l, i)
-                if i >= LAG or l + 1 == L:
-                    feed_transpose()
-                if l + 1 == L and i >= 4 and len(pending) > 2:
-                    feed_transpose()
-                pending.append((l, i))
-                if i % 2 == 1:
-                    feed_quant(1)
-                if l + 2 < L and i >= 4:
-                    front(l + 2, i - 4)
+                acts(i)
+                if i < G_TILES:
+                    loss(l, i)
+                else:
+                    later(1, loss, l, i)
+                later(R_LAG, finish_tile, l, i)
+                tick()
 
-        transpose_a(0)
-        transpose_a(1)
-        permute_r()
-        front(0, 0)
-        front(0, 2)
-        transpose_a(2)
-        transpose_a(3)
-        front(0, 1)
-        front(0, 3)
-        slot_a(0, -1)
+        def first_scores(l):
+            scores(l, 0)
+            scores(l, 1)
+
+        def first_matmuls(l):
+            matmul_1(l, 0)
+            matmul_1(l, 1)
+
+        def sigmoids_behind(l, i):
+            if i % 2 == 0 and i > 0:
+                sigmoid(l, i - 2)
+                sigmoid(l, i - 1)
+
+        chunks = [(l, c) for l in AU_ACT for c in range(TILES)]
+
+        def feed_chunk(n=1):
+            for k in range(n):
+                if chunks:
+                    scale_a_chunk(*chunks.pop(0))
+
+        for l in AU_ACT:
+            make_diagonals(l)
         for j in range(PAIRS):
-            log(0, j)
-        for part in range(4):
-            front(1, part)
-        for l in range(L):
-            if l + 1 < L:
-                slot_a(l + 1, l)
-            else:
-                scores(l, 0)
-                scores(l, 1)
-            slot_b(l)
-        while pending or quants:
-            feed_transpose()
-            feed_quant(0 if not pending else 1)
+            transpose_a(j)
+        permute_r_words()
+        scale_a(0, 0, 0, 256)
+        quant_a(0, 0, 0, 256)
+        permute_r_scales()
+        feed_chunk(C0)
+        first_matmuls(0)
+        scale_a(0, 0, 256, 256)
+        quant_a(0, 0, 256, 256)
+        feed_chunk(C1)
+        scale_t(0, 0)
+        scale_t(0, 1)
+        matmul_1(0, 2)
+        matmul_1(0, 3)
+        quant_t(0, 0)
+        feed_chunk(C2)
+        sigmoid(0, 0)
+        sigmoid(0, 1)
+        scale_a(0, 1)
+        quant_a(0, 1)
+        for i in range(2, TILES):
+            scale_t(0, i)
+            if i + 2 < TILES:
+                matmul_1(0, i + 2)
+            feed_chunk()
+            if i % 2 == 0 and i > 2:
+                quant_t(0, i // 2 - 1)
+                sigmoid(0, i - 2)
+                sigmoid(0, i - 1)
+        quant_t(0, 3)
+        front(1)
+        first_matmuls(1)
+        sigmoid(0, 6)
+        sigmoid(0, 7)
 
+        def acts_a1(i):
+            feed_chunk()
+            sigmoids_behind(1, i)
 
-def GP_ENGINE(nc, l, i):
-    return nc.gpsimd if not (l == L - 1 and i >= 6) else nc.vector
+        slot_a(1, acts_a1)
+        front(2)
+        first_matmuls(2)
+        sigmoid(1, 6)
+        sigmoid(1, 7)
+
+        def acts_a2(i):
+            log(i // PAIRS, i % PAIRS)
+            feed_chunk()
+            if i == 7:
+                first_scores(0)
+
+        slot_a(2, acts_a2)
+        front(3)
+
+        def acts_b0(i):
+            sigmoid(2, i)
+            if i == 6:
+                first_matmuls(3)
+
+        slot_b(0, acts_b0)
+
+        def acts_a3(i):
+            sigmoids_behind(3, i)
+            if i == 5:
+                first_scores(1)
+
+        slot_a(3, acts_a3)
+        sigmoid(3, 6)
+        sigmoid(3, 7)
+
+        def acts_b1(i):
+            if i < PAIRS:
+                log(2, i)
+            if i == 7:
+                first_scores(2)
+
+        def acts_b2(i):
+            if i < PAIRS:
+                log(3, i)
+            if i == 7:
+                first_scores(3)
+
+        slot_b(1, acts_b1)
+        slot_b(2, acts_b2)
+        slot_b(3, lambda i: None)
+        while due:
+            tick()

@@ -19,10 +19,12 @@ ACTF = mybir.ActivationFunctionType
 TILES = N // 128
 PAIRS = TILES // 2
 DELTA = 2.0 ** -63
-G_TILES = 6
+G_TILES = {0: 7, 1: 7, 2: 7, 3: 6}
+WARM = True
+LEAD = {0: 2, 1: 4, 2: 4, 3: 4}
 AU_ACT = (1, 2)
 C0, C1, C2 = 0, 2, 4
-R_LAG, T_LAG, Q_LAG = 3, 3, 4
+LAGS = {0: (3, 2, 4), 1: (3, 2, 4), 2: (3, 2, 4), 3: (3, 2, 3)}
 
 
 def tile_dualdomaindedicomlogisticloss_x2_kernel(
@@ -41,6 +43,8 @@ def tile_dualdomaindedicomlogisticloss_x2_kernel(
         bs = keep.tile([128, P], U8, name="bs", align_bytes=64)
         nc.vector.memset(rs_raw[:].bitcast(I32), 0)
         nc.vector.memset(bs[:].bitcast(I32), 0)
+        uv_rows = keep.tile([128, D], BF16, name="uv_rows")
+        nc.vector.memset(uv_rows[:].bitcast(I32), 0)
         ident = keep.tile([128, 128], F32, name="ident")
         make_identity(nc, ident[:])
 
@@ -53,14 +57,12 @@ def tile_dualdomaindedicomlogisticloss_x2_kernel(
             if j == 0:
                 nc.sync.dma_start(out=rw_raw[:].bitcast(I32), in_=r_words[0].bitcast(I32))
         bw = keep.tile([128, 2 * P], U8, name="bw", align_bytes=64)
-        u_sb = keep.tile([128, L, 4], BF16, name="u_sb")
-        v_sb = keep.tile([128, L, 4], BF16, name="v_sb")
-        nc.scalar.dma_start(out=u_sb[:], in_=u.rearrange("l (p t) -> p l t", t=4))
+        nc.scalar.dma_start(out=uv_rows[0:L, :], in_=u)
+        nc.scalar.dma_start(out=uv_rows[L : 2 * L, :], in_=v)
         for q in range(4):
             nc.scalar.dma_start(
                 out=rs_raw[32 * q : 32 * q + 4, :].bitcast(I32), in_=r_scales[0, 4 * q : 4 * q + 4, :].bitcast(I32)
             )
-        nc.scalar.dma_start(out=v_sb[:], in_=v.rearrange("l (p t) -> p l t", t=4))
         warm = keep.tile([128, 1], F32, name="warm")
         nc.vector.memset(warm[:], 0.0)
         nc.scalar.activation(out=warm[:], in_=warm[:], func=ACTF.Sigmoid)
@@ -72,8 +74,10 @@ def tile_dualdomaindedicomlogisticloss_x2_kernel(
         x_sb = []
         for l in range(L):
             x_l = keep.tile([128, TILES, P], BF16, name="x%d" % l)
-            nc.sync.dma_start(out=x_l[:], in_=x[l].rearrange("(i p) k -> p i k", p=128))
             x_sb.append(x_l)
+
+        def load_x(l):
+            nc.scalar.dma_start(out=x_sb[l][:], in_=x[l].rearrange("(i p) k -> p i k", p=128))
 
         rw = keep.tile([128, 4, 256], U8, name="rw", align_bytes=64)
         rs = keep.tile([128, 4, 128], U8, name="rs", align_bytes=64)
@@ -86,6 +90,15 @@ def tile_dualdomaindedicomlogisticloss_x2_kernel(
 
         def permute_r_scales():
             nc.vector.tensor_copy(out=rs[:], in_=rs_raw[:].rearrange("p (m t) -> p t m", t=4))
+
+        uv = keep.tile([128, 2 * L, 4], BF16, name="uv")
+
+        def transpose_uv():
+            ps = psum.tile([128, 2, 128], F32, name="ps_uv", tag="s1")
+            words = uv_rows[:].bitcast(F32)
+            for k in range(2):
+                nc.tensor.transpose(ps[:, k, :], words[:, k : 256 : 2], ident[:])
+            nc.vector.tensor_copy(out=uv[:].bitcast(F32), in_=ps[:, :, 0 : 2 * L].rearrange("p k r -> p r k"))
 
         aT = []
         for h in range(2):
@@ -113,7 +126,7 @@ def tile_dualdomaindedicomlogisticloss_x2_kernel(
             nc.vector.tensor_tensor(
                 out=st["auq", l, h][:, cols, :],
                 in0=aT[h][:, cols, :],
-                in1=u_sb[:, l, :].unsqueeze(1).to_broadcast([128, w, 4]),
+                in1=uv[:, l, :].unsqueeze(1).to_broadcast([128, w, 4]),
                 op=ALU.mult,
             )
 
@@ -123,7 +136,7 @@ def tile_dualdomaindedicomlogisticloss_x2_kernel(
                 nc.gpsimd.tensor_scalar(
                     out=diag[:, t, :],
                     in0=ident[:],
-                    scalar1=u_sb[:, l, t : t + 1],
+                    scalar1=uv[:, l, t : t + 1],
                     scalar2=0.0,
                     op0=ALU.mult,
                     op1=ALU.add,
@@ -184,7 +197,7 @@ def tile_dualdomaindedicomlogisticloss_x2_kernel(
             nc.vector.tensor_tensor(
                 out=tvq[:, n0 : n0 + 128, :],
                 in0=st["t", l, i][:].rearrange("p t n -> p n t"),
-                in1=v_sb[:, l, :].unsqueeze(1).to_broadcast([128, 128, 4]),
+                in1=uv[:, L + l, :].unsqueeze(1).to_broadcast([128, 128, 4]),
                 op=ALU.mult,
             )
 
@@ -196,25 +209,26 @@ def tile_dualdomaindedicomlogisticloss_x2_kernel(
             )
             st["tv", l, j] = (c, s)
 
-        def matmul_2(l, i, tag):
+        def matmul_2(l, i, tag, times=1):
             c, s = st["tv", l, i // 2]
             n0 = 128 * (i % 2)
             ps = psum.tile([128, P], F32, name="ps_" + tag, tag=tag)
-            nc.tensor.matmul_mx(
-                out=ps[:],
-                lhsT=c[:, n0 : n0 + 128].bitcast(FP8),
-                lhsT_scale=s[:, n0 : n0 + 128],
-                rhs=bw[:].bitcast(FP4),
-                rhs_scale=bs[:],
-                start=True,
-                stop=True,
-            )
+            for k in range(times):
+                nc.tensor.matmul_mx(
+                    out=ps[:],
+                    lhsT=c[:, n0 : n0 + 128].bitcast(FP8),
+                    lhsT_scale=s[:, n0 : n0 + 128],
+                    rhs=bw[:].bitcast(FP4),
+                    rhs_scale=bs[:],
+                    start=True,
+                    stop=True,
+                )
             return ps
 
         def sigmoid(l, i):
             ps = matmul_2(l, i, "s1")
             if i % 2 == 0:
-                sg = work.tile([128, 2, P], F32, name="sg", bufs=14)
+                sg = work.tile([128, 2, P], F32, name="sg", bufs=12)
                 st["sg", l, i // 2] = sg
             nc.scalar.activation(out=st["sg", l, i // 2][:, i % 2, :], in_=ps[:], func=ACTF.Sigmoid, scale=-1.0)
 
@@ -223,13 +237,14 @@ def tile_dualdomaindedicomlogisticloss_x2_kernel(
             nc.scalar.activation(out=sg[:], in_=sg[:], func=ACTF.Ln, bias=DELTA)
 
         def scores(l, i):
-            st["s", l, i] = matmul_2(l, i, "s2")
+            tag = "s2" if l == 0 else ("s2", "s2", "t", "t", "s1", "s1")[(8 * (l - 1) + i) % 6]
+            st["s", l, i] = matmul_2(l, i, tag, 2 if l > 0 and WARM else 1)
 
         def loss_parts(l, i):
             ps = st["s", l, i]
-            xs = work.tile([128, P], F32, name="xs", bufs=5)
+            xs = work.tile([128, P], F32, name="xs", bufs=6)
             nc.vector.tensor_tensor(out=xs[:], in0=ps[:], in1=x_sb[l][:, i, :], op=ALU.mult)
-            sp = work.tile([128, P], F32, name="sp", bufs=5)
+            sp = work.tile([128, P], F32, name="sp", bufs=6)
             nc.vector.scalar_tensor_tensor(
                 out=sp[:], in0=st["sg", l, i // 2][:, i % 2, :], scalar=-1.0, in1=ps[:], op0=ALU.mult, op1=ALU.max
             )
@@ -238,10 +253,10 @@ def tile_dualdomaindedicomlogisticloss_x2_kernel(
         def loss(l, i):
             sp, xs = st["parts", l, i]
             if i % 2 == 0:
-                res = work.tile([128, 2, P], F32, name="res", bufs=4)
+                res = work.tile([128, 2, P], F32, name="res", bufs=6)
                 st["res", l, i // 2] = res
             res = st["res", l, i // 2]
-            engine = nc.vector if i >= G_TILES else nc.gpsimd
+            engine = nc.vector if i >= G_TILES[l] else nc.gpsimd
             engine.tensor_tensor(out=res[:, i % 2, :], in0=sp[:], in1=xs[:], op=ALU.subtract)
             if i % 2 == 1:
                 n0 = 128 * (i - 1)
@@ -250,7 +265,7 @@ def tile_dualdomaindedicomlogisticloss_x2_kernel(
                 )
 
         def round_out(l, i):
-            rb = work.tile([128, P], BF16, name="rb", bufs=4)
+            rb = work.tile([128, P], BF16, name="rb", bufs=6)
             nc.scalar.copy(out=rb[:], in_=st["res", l, i // 2][:, i % 2, :])
             st["rb", l, i] = rb
 
@@ -305,11 +320,11 @@ def tile_dualdomaindedicomlogisticloss_x2_kernel(
         def finish_tile(l, i):
             round_out(l, i)
             if i % 2 == 1:
-                later(T_LAG, finish_pair, l, i // 2)
+                later(LAGS[l][1], finish_pair, l, i // 2)
 
         def finish_pair(l, j):
             transpose_out(l, j)
-            later(Q_LAG, quant_out, l, j)
+            later(LAGS[l][2], quant_out, l, j)
 
         def front(l):
             if l not in AU_ACT:
@@ -332,19 +347,21 @@ def tile_dualdomaindedicomlogisticloss_x2_kernel(
         def slot_b(l, acts):
             for i in range(TILES):
                 loss_parts(l, i)
-                if i + 2 < TILES:
-                    scores(l, i + 2)
+                if i + LEAD[l] < TILES:
+                    scores(l, i + LEAD[l])
+                elif l > 0 and l + 1 < L:
+                    scores(l + 1, i + LEAD[l] - TILES)
                 acts(i)
-                if i < G_TILES:
+                if i < G_TILES[l]:
                     loss(l, i)
                 else:
                     later(1, loss, l, i)
-                later(R_LAG, finish_tile, l, i)
+                later(LAGS[l][0], finish_tile, l, i)
                 tick()
 
         def first_scores(l):
-            scores(l, 0)
-            scores(l, 1)
+            for i in range(LEAD[l]):
+                scores(l, i)
 
         def first_matmuls(l):
             matmul_1(l, 0)
@@ -362,11 +379,15 @@ def tile_dualdomaindedicomlogisticloss_x2_kernel(
                 if chunks:
                     scale_a_chunk(*chunks.pop(0))
 
+        permute_r_words()
+        transpose_a(0)
+        transpose_uv()
         for l in AU_ACT:
             make_diagonals(l)
-        for j in range(PAIRS):
+        for j in range(1, PAIRS):
             transpose_a(j)
-        permute_r_words()
+        for l in range(L):
+            load_x(l)
         scale_a(0, 0, 0, 256)
         quant_a(0, 0, 0, 256)
         permute_r_scales()
@@ -428,24 +449,19 @@ def tile_dualdomaindedicomlogisticloss_x2_kernel(
 
         def acts_a3(i):
             sigmoids_behind(3, i)
-            if i == 5:
-                first_scores(1)
 
         slot_a(3, acts_a3)
+        first_scores(1)
         sigmoid(3, 6)
         sigmoid(3, 7)
 
         def acts_b1(i):
             if i < PAIRS:
                 log(2, i)
-            if i == 7:
-                first_scores(2)
 
         def acts_b2(i):
             if i < PAIRS:
                 log(3, i)
-            if i == 7:
-                first_scores(3)
 
         slot_b(1, acts_b1)
         slot_b(2, acts_b2)

@@ -19,12 +19,23 @@ ACTF = mybir.ActivationFunctionType
 TILES = N // 128
 PAIRS = TILES // 2
 DELTA = 2.0 ** -63
-G_TILES = {0: 7, 1: 7, 2: 7, 3: 6}
+V_TILES = ((), (7,), (7,), (7,))
 WARM = True
 LEAD = {0: 2, 1: 4, 2: 4, 3: 4}
 AU_ACT = (1, 2)
-C0, C1, C2 = 0, 2, 4
-LAGS = {0: (3, 2, 4), 1: (3, 2, 4), 2: (3, 2, 4), 3: (3, 2, 3)}
+C0, C1, C2 = 0, 4, 2
+LAGS = {0: (3,2,5), 1: (3,2,5), 2: (3,2,5), 3: (2,2,2)}
+Q_TILES = {0: 4, 1: 4, 2: 4, 3: 4}
+T_TILES = {0: 2, 1: 2, 2: 4, 3: 4}
+D_LAG = 1
+RW_FIRST = True
+HEAD1 = False
+EARLY_T = False
+S0, S01, S1, S12, S2_FROM, S2, S3, S31 = 2, 4, 1, 2, 0, 1, 1, 8
+LOG_A2 = {1: (0, 0), 3: (0, 4), 5: (1, 0), 7: (1, 4)}
+LOG_B1 = {0: (2, 0), 2: (2, 4)}
+LOG_B2 = {0: (3, 0), 2: (3, 4)}
+R_TILES = {0: 1, 1: 1, 2: 1, 3: 1}
 
 
 def tile_dualdomaindedicomlogisticloss_x2_kernel(
@@ -116,6 +127,16 @@ def tile_dualdomaindedicomlogisticloss_x2_kernel(
             src = ps[:].rearrange("p i k n -> p i n k")
             nc.scalar.copy(out=dst, in_=src)
 
+        def transpose_a_tile(j, i):
+            ps = psum.tile([128, 2, 128], F32, name="ps_a1", tag="o")
+            words = a_sb[j][:].bitcast(F32)
+            for k in range(2):
+                nc.tensor.transpose(ps[:, k, :], words[:, i, k : 256 : 2], ident[:])
+            c0 = 256 * (j % 2) + 128 * i
+            nc.scalar.copy(
+                out=aT[j // 2][:, c0 : c0 + 128, :].bitcast(F32), in_=ps[:].rearrange("p k n -> p n k")
+            )
+
         st = {}
 
         def scale_a(l, h, c0=0, w=512):
@@ -147,6 +168,7 @@ def tile_dualdomaindedicomlogisticloss_x2_kernel(
             if c % 4 == 0:
                 auq = work.tile([128, 512, 4], BF16, name="auq", bufs=4, align_bytes=64)
                 st["auq", l, c // 4] = auq
+            st["chunk", l, c] = True
             n0 = 128 * (c % 4)
             ps = psum.tile([128, 4, 128], F32, name="ps_u", tag="o" if c % 2 else "s2")
             for t in range(4):
@@ -164,6 +186,8 @@ def tile_dualdomaindedicomlogisticloss_x2_kernel(
                 c = work.tile([128, 512], U32, name="au_c", bufs=2, align_bytes=64)
                 s = work.tile([128, 512], U8, name="au_s", bufs=2, align_bytes=64)
                 st["au", l, h] = (c, s)
+            if l in AU_ACT:
+                assert all(("chunk", l, 4 * h + k) in st for k in range(4))
             c, s = st["au", l, h]
             cols = slice(c0, c0 + w)
             nc.vector.quantize_mx(
@@ -189,29 +213,34 @@ def tile_dualdomaindedicomlogisticloss_x2_kernel(
             st["t", l, i] = ps
 
         def scale_t(l, i):
-            if i % 2 == 0:
-                tvq = work.tile([128, 256, 4], BF16, name="tvq", bufs=3, align_bytes=64)
-                st["tvq", l, i // 2] = tvq
-            tvq = st["tvq", l, i // 2]
-            n0 = 128 * (i % 2)
+            if i % 4 == 0:
+                tvq = work.tile([128, 512, 4], BF16, name="tvq", bufs=2, align_bytes=64)
+                st["tvq", l, i // 4] = tvq
+            n0 = 128 * (i % 4)
             nc.vector.tensor_tensor(
-                out=tvq[:, n0 : n0 + 128, :],
+                out=st["tvq", l, i // 4][:, n0 : n0 + 128, :],
                 in0=st["t", l, i][:].rearrange("p t n -> p n t"),
                 in1=uv[:, L + l, :].unsqueeze(1).to_broadcast([128, 128, 4]),
                 op=ALU.mult,
             )
 
-        def quant_t(l, j):
-            c = work.tile([128, 256], U32, name="tv_c", bufs=12, align_bytes=64)
-            s = work.tile([128, 256], U8, name="tv_s", bufs=12, align_bytes=64)
+        def quant_t(l, first, count):
+            h = first // 4
+            if first % 4 == 0:
+                c = work.tile([128, 512], U32, name="tv_c", bufs=6, align_bytes=64)
+                s = work.tile([128, 512], U8, name="tv_s", bufs=6, align_bytes=64)
+                st["tv", l, h] = (c, s)
+            c, s = st["tv", l, h]
+            cols = slice(128 * (first % 4), 128 * (first % 4 + count))
             nc.vector.quantize_mx(
-                out=c[:].bitcast(FP8), scales=s[:], in_=st["tvq", l, j][:].rearrange("p n t -> p (n t)")
+                out=c[:, cols].bitcast(FP8),
+                scales=s[:, cols],
+                in_=st["tvq", l, h][:, cols, :].rearrange("p n t -> p (n t)"),
             )
-            st["tv", l, j] = (c, s)
 
         def matmul_2(l, i, tag, times=1):
-            c, s = st["tv", l, i // 2]
-            n0 = 128 * (i % 2)
+            c, s = st["tv", l, i // 4]
+            n0 = 128 * (i % 4)
             ps = psum.tile([128, P], F32, name="ps_" + tag, tag=tag)
             for k in range(times):
                 nc.tensor.matmul_mx(
@@ -227,14 +256,19 @@ def tile_dualdomaindedicomlogisticloss_x2_kernel(
 
         def sigmoid(l, i):
             ps = matmul_2(l, i, "s1")
-            if i % 2 == 0:
-                sg = work.tile([128, 2, P], F32, name="sg", bufs=12)
-                st["sg", l, i // 2] = sg
-            nc.scalar.activation(out=st["sg", l, i // 2][:, i % 2, :], in_=ps[:], func=ACTF.Sigmoid, scale=-1.0)
+            if i % 4 == 0:
+                sg = work.tile([128, 4, P], F32, name="sg", bufs=7)
+                st["sg", l, i // 4] = sg
+            nc.scalar.activation(out=st["sg", l, i // 4][:, i % 4, :], in_=ps[:], func=ACTF.Sigmoid, scale=-1.0)
 
-        def log(l, j):
-            sg = st["sg", l, j]
-            nc.scalar.activation(out=sg[:], in_=sg[:], func=ACTF.Ln, bias=DELTA)
+            st["sig", l, i] = True
+
+        def log(l, first, count=4):
+            sg = st["sg", l, first // 4][:, first % 4 : first % 4 + count, :]
+            assert all(("sig", l, k) in st for k in range(first, first + count))
+            nc.scalar.activation(out=sg, in_=sg, func=ACTF.Ln, bias=DELTA)
+            for k in range(first, first + count):
+                st["log", l, k] = True
 
         def scores(l, i):
             tag = "s2" if l == 0 else ("s2", "s2", "t", "t", "s1", "s1")[(8 * (l - 1) + i) % 6]
@@ -242,11 +276,12 @@ def tile_dualdomaindedicomlogisticloss_x2_kernel(
 
         def loss_parts(l, i):
             ps = st["s", l, i]
+            assert ("log", l, i) in st
             xs = work.tile([128, P], F32, name="xs", bufs=6)
             nc.vector.tensor_tensor(out=xs[:], in0=ps[:], in1=x_sb[l][:, i, :], op=ALU.mult)
             sp = work.tile([128, P], F32, name="sp", bufs=6)
             nc.vector.scalar_tensor_tensor(
-                out=sp[:], in0=st["sg", l, i // 2][:, i % 2, :], scalar=-1.0, in1=ps[:], op0=ALU.mult, op1=ALU.max
+                out=sp[:], in0=st["sg", l, i // 4][:, i % 4, :], scalar=-1.0, in1=ps[:], op0=ALU.mult, op1=ALU.max
             )
             st["parts", l, i] = (sp, xs)
 
@@ -256,7 +291,7 @@ def tile_dualdomaindedicomlogisticloss_x2_kernel(
                 res = work.tile([128, 2, P], F32, name="res", bufs=6)
                 st["res", l, i // 2] = res
             res = st["res", l, i // 2]
-            engine = nc.vector if i >= G_TILES[l] else nc.gpsimd
+            engine = nc.vector if i in V_TILES[l] else nc.gpsimd
             engine.tensor_tensor(out=res[:, i % 2, :], in0=sp[:], in1=xs[:], op=ALU.subtract)
             if i % 2 == 1:
                 n0 = 128 * (i - 1)
@@ -264,42 +299,50 @@ def tile_dualdomaindedicomlogisticloss_x2_kernel(
                     out=out_0[l, n0 : n0 + 256, :].rearrange("(i p) k -> p i k", p=128), in_=res[:]
                 )
 
-        def round_out(l, i):
-            rb = work.tile([128, P], BF16, name="rb", bufs=6)
-            nc.scalar.copy(out=rb[:], in_=st["res", l, i // 2][:, i % 2, :])
-            st["rb", l, i] = rb
+        def round_out(l, first, count):
+            j = first // 2
+            if first % 2 == 0:
+                rb = work.tile([128, 2, P], BF16, name="rb", bufs=3)
+                st["rb", l, j] = rb
+            part = slice(first % 2, first % 2 + count)
+            nc.scalar.copy(out=st["rb", l, j][:, part, :], in_=st["res", l, j][:, part, :])
 
         def transpose_out(l, j):
-            oq = work.tile([128, 256, 4], BF16, name="oq", bufs=4, align_bytes=64)
+            if j % 2 == 0:
+                oq = work.tile([128, 512, 4], BF16, name="oq", bufs=3, align_bytes=64)
+                st["oq", l, j // 2] = oq
             ps = psum.tile([128, 2, 2, 128], F32, name="ps_o", tag="o")
             for i in range(2):
-                words = st["rb", l, 2 * j + i][:].bitcast(F32)
+                words = st["rb", l, j][:, i, :].bitcast(F32)
                 for k in range(2):
                     nc.tensor.transpose(ps[:, i, k, :], words[:, k : 256 : 2], ident[:])
+            n0 = 256 * (j % 2)
             nc.scalar.copy(
-                out=oq[:].bitcast(F32).rearrange("p (i n) k -> p i n k", i=2), in_=ps[:].rearrange("p i k n -> p i n k")
+                out=st["oq", l, j // 2][:, n0 : n0 + 256, :].bitcast(F32).rearrange("p (i n) k -> p i n k", i=2),
+                in_=ps[:].rearrange("p i k n -> p i n k"),
             )
-            st["oq", l, j] = oq
 
-        def quant_out(l, j):
-            if j == 0:
+        def quant_out(l, first, count):
+            h = first // 4
+            if first == 0:
                 o_s = work.tile([128, N], U8, name="o_s", bufs=2, align_bytes=64)
                 st["o_s", l] = o_s
-            if j % 2 == 0:
-                o_c = work.tile([128, 512], U32, name="o_c", bufs=4, align_bytes=64)
-                st["o_c", l, j // 2] = o_c
+            if first % 4 == 0:
+                o_c = work.tile([128, 512], U32, name="o_c", bufs=3, align_bytes=64)
+                st["o_c", l, h] = o_c
             o_s = st["o_s", l]
-            o_c = st["o_c", l, j // 2]
-            c0 = 256 * (j % 2)
+            o_c = st["o_c", l, h]
+            c0, w = 128 * (first % 4), 128 * count
             nc.vector.quantize_mx(
-                out=o_c[:, c0 : c0 + 256].bitcast(FP8),
-                scales=o_s[:, 256 * j : 256 * j + 256],
-                in_=st["oq", l, j][:].rearrange("p n t -> p (n t)"),
+                out=o_c[:, c0 : c0 + w].bitcast(FP8),
+                scales=o_s[:, 128 * first : 128 * first + w],
+                in_=st["oq", l, h][:, c0 : c0 + w, :].rearrange("p n t -> p (n t)"),
             )
-            if j % 2 == 1:
-                m0 = N * l + 512 * (j // 2)
-                nc.sync.dma_start(out=words_out[:, 4 * m0 : 4 * m0 + 2048].bitcast(I32), in_=o_c[:].bitcast(I32))
-            if j == PAIRS - 1:
+            m0 = N * l + 128 * first
+            nc.sync.dma_start(
+                out=words_out[:, 4 * m0 : 4 * (m0 + w)].bitcast(I32), in_=o_c[:, c0 : c0 + w].bitcast(I32)
+            )
+            if first + count == TILES:
                 for q in range(4):
                     nc.sync.dma_start(
                         out=out_2[0, 4 * q : 4 * q + 4, N * l : N * l + N].bitcast(I32),
@@ -308,6 +351,8 @@ def tile_dualdomaindedicomlogisticloss_x2_kernel(
 
         clock = [0]
         due = {}
+        sigmoids = []
+        chunks = [(l, c) for l in AU_ACT for c in range(TILES)]
 
         def later(steps, fn, *args):
             due.setdefault(clock[0] + steps, []).append((fn, args))
@@ -317,14 +362,28 @@ def tile_dualdomaindedicomlogisticloss_x2_kernel(
                 fn(*args)
             clock[0] += 1
 
+        def feed_chunk(n=1):
+            for k in range(n):
+                if chunks:
+                    scale_a_chunk(*chunks.pop(0))
+
+        def feed_sigmoid(n=1):
+            for k in range(n):
+                if sigmoids:
+                    sigmoid(*sigmoids.pop(0))
+
         def finish_tile(l, i):
-            round_out(l, i)
+            n = R_TILES[l]
+            if i % n == n - 1:
+                round_out(l, i + 1 - n, n)
             if i % 2 == 1:
                 later(LAGS[l][1], finish_pair, l, i // 2)
 
         def finish_pair(l, j):
             transpose_out(l, j)
-            later(LAGS[l][2], quant_out, l, j)
+            n = Q_TILES[l]
+            if (2 * j + 2) % n == 0:
+                later(LAGS[l][2], quant_out, l, 2 * j + 2 - n, n)
 
         def front(l):
             if l not in AU_ACT:
@@ -333,16 +392,19 @@ def tile_dualdomaindedicomlogisticloss_x2_kernel(
             quant_a(l, 0)
             quant_a(l, 1)
 
-        def slot_a(l, acts):
-            for i in range(TILES):
+        def slot_a(l, acts, first=0):
+            n = T_TILES[l]
+            for i in range(first, TILES):
                 scale_t(l, i)
                 if i + 2 < TILES:
                     matmul_1(l, i + 2)
-                if i % 2 == 0 and i > 0:
-                    quant_t(l, i // 2 - 1)
+                if i % n == 0 and i > first:
+                    quant_t(l, i - n, n)
+                    sigmoids.extend([(l, k) for k in range(i - n, i)])
                 acts(i)
                 tick()
-            quant_t(l, PAIRS - 1)
+            quant_t(l, TILES - n, n)
+            sigmoids.extend([(l, k) for k in range(TILES - n, TILES)])
 
         def slot_b(l, acts):
             for i in range(TILES):
@@ -352,116 +414,130 @@ def tile_dualdomaindedicomlogisticloss_x2_kernel(
                 elif l > 0 and l + 1 < L:
                     scores(l + 1, i + LEAD[l] - TILES)
                 acts(i)
-                if i < G_TILES[l]:
+                if i not in V_TILES[l]:
                     loss(l, i)
                 else:
-                    later(1, loss, l, i)
+                    later(D_LAG, loss, l, i)
                 later(LAGS[l][0], finish_tile, l, i)
                 tick()
 
-        def first_scores(l):
-            for i in range(LEAD[l]):
+        def first_scores(l, count):
+            for i in range(count):
                 scores(l, i)
 
         def first_matmuls(l):
             matmul_1(l, 0)
             matmul_1(l, 1)
 
-        def sigmoids_behind(l, i):
-            if i % 2 == 0 and i > 0:
-                sigmoid(l, i - 2)
-                sigmoid(l, i - 1)
-
-        chunks = [(l, c) for l in AU_ACT for c in range(TILES)]
-
-        def feed_chunk(n=1):
-            for k in range(n):
-                if chunks:
-                    scale_a_chunk(*chunks.pop(0))
-
-        permute_r_words()
-        transpose_a(0)
-        transpose_uv()
+        if RW_FIRST:
+            permute_r_words()
+        if HEAD1:
+            transpose_a_tile(0, 0)
+            transpose_uv()
+            transpose_a_tile(0, 1)
+        else:
+            transpose_a(0)
+            transpose_uv()
         for l in AU_ACT:
             make_diagonals(l)
         for j in range(1, PAIRS):
             transpose_a(j)
         for l in range(L):
             load_x(l)
-        scale_a(0, 0, 0, 256)
-        quant_a(0, 0, 0, 256)
-        permute_r_scales()
+        if HEAD1:
+            scale_a(0, 0, 0, 128)
+            scale_a(0, 0, 128, 128)
+            quant_a(0, 0, 0, 128)
+            if not RW_FIRST:
+                permute_r_words()
+            permute_r_scales()
+            quant_a(0, 0, 128, 128)
+        else:
+            scale_a(0, 0, 0, 256)
+            if not RW_FIRST:
+                permute_r_words()
+            quant_a(0, 0, 0, 256)
+            permute_r_scales()
         feed_chunk(C0)
         first_matmuls(0)
         scale_a(0, 0, 256, 256)
-        quant_a(0, 0, 256, 256)
-        feed_chunk(C1)
-        scale_t(0, 0)
-        scale_t(0, 1)
+        if EARLY_T:
+            scale_t(0, 0)
+            scale_t(0, 1)
+            quant_a(0, 0, 256, 256)
+        else:
+            quant_a(0, 0, 256, 256)
+            feed_chunk(C1)
+            scale_t(0, 0)
+            scale_t(0, 1)
         matmul_1(0, 2)
         matmul_1(0, 3)
-        quant_t(0, 0)
+        quant_t(0, 0, 2)
         feed_chunk(C2)
         sigmoid(0, 0)
         sigmoid(0, 1)
         scale_a(0, 1)
         quant_a(0, 1)
-        for i in range(2, TILES):
-            scale_t(0, i)
-            if i + 2 < TILES:
-                matmul_1(0, i + 2)
+
+        def acts_a0(i):
             feed_chunk()
-            if i % 2 == 0 and i > 2:
-                quant_t(0, i // 2 - 1)
-                sigmoid(0, i - 2)
-                sigmoid(0, i - 1)
-        quant_t(0, 3)
+            feed_sigmoid(S0)
+
+        slot_a(0, acts_a0, 2)
         front(1)
         first_matmuls(1)
-        sigmoid(0, 6)
-        sigmoid(0, 7)
+        feed_sigmoid(S01)
 
         def acts_a1(i):
             feed_chunk()
-            sigmoids_behind(1, i)
+            feed_sigmoid(S1)
 
         slot_a(1, acts_a1)
         front(2)
         first_matmuls(2)
-        sigmoid(1, 6)
-        sigmoid(1, 7)
+        feed_sigmoid(S12)
 
         def acts_a2(i):
-            log(i // PAIRS, i % PAIRS)
-            feed_chunk()
-            if i == 7:
-                first_scores(0)
+            if sigmoids and sigmoids[0][0] < 2:
+                feed_sigmoid(2)
+            elif i in LOG_A2:
+                log(*LOG_A2[i])
+            if i == 6:
+                first_scores(0, 2)
 
         slot_a(2, acts_a2)
         front(3)
 
         def acts_b0(i):
-            sigmoid(2, i)
+            if i == 0:
+                for k in (0, 4):
+                    if (1, k) not in LOG_A2.values():
+                        log(1, k)
+            if i >= S2_FROM:
+                feed_sigmoid(S2)
             if i == 6:
                 first_matmuls(3)
 
         slot_b(0, acts_b0)
 
         def acts_a3(i):
-            sigmoids_behind(3, i)
+            feed_sigmoid(S3)
+            if i == 5:
+                first_scores(1, 2)
 
         slot_a(3, acts_a3)
-        first_scores(1)
-        sigmoid(3, 6)
-        sigmoid(3, 7)
+        for i in range(2, LEAD[1]):
+            scores(1, i)
+        feed_sigmoid(S31)
 
         def acts_b1(i):
-            if i < PAIRS:
-                log(2, i)
+            feed_sigmoid(2)
+            if i in LOG_B1:
+                log(*LOG_B1[i])
 
         def acts_b2(i):
-            if i < PAIRS:
-                log(3, i)
+            if i in LOG_B2:
+                log(*LOG_B2[i])
 
         slot_b(1, acts_b1)
         slot_b(2, acts_b2)

from contextlib import ExitStack

import concourse.mybir as mybir
from concourse.masks import make_identity

L, N, D, P = 4, 1024, 512, 512
FLOPS = 2 * L * N * D * D + 2 * L * N * D * P

F32 = mybir.dt.float32
BF16 = mybir.dt.bfloat16
I32 = mybir.dt.int32
U32 = mybir.dt.uint32
U8 = mybir.dt.uint8
FP8 = mybir.dt.float8_e4m3fn_x4
FP4 = mybir.dt.float4_e2m1fn_x4
ALU = mybir.AluOpType
ACTF = mybir.ActivationFunctionType

TILES = N // 128
PAIRS = TILES // 2
DELTA = 2.0 ** -63
V_TILES = ((), (7,), (7,), (7,))
WARM = True
LEAD = {0: 2, 1: 4, 2: 4, 3: 4}
AU_ACT = (1, 2)
C0, C1, C2 = 0, 4, 2
LAGS = {0: (3,2,5), 1: (3,2,5), 2: (3,2,5), 3: (2,2,2)}
Q_TILES = {0: 4, 1: 4, 2: 4, 3: 4}
T_TILES = {0: 2, 1: 2, 2: 4, 3: 4}
D_LAG = 1
RW_FIRST = True
HEAD1 = False
EARLY_T = False
S0, S01, S1, S12, S2_FROM, S2, S3, S31 = 2, 4, 1, 2, 0, 1, 1, 8
LOG_A2 = {1: (0, 0), 3: (0, 4), 5: (1, 0), 7: (1, 4)}
LOG_B1 = {0: (2, 0), 2: (2, 4)}
LOG_B2 = {0: (3, 0), 2: (3, 4)}
R_TILES = {0: 1, 1: 1, 2: 1, 3: 1}


def tile_dualdomaindedicomlogisticloss_x2_kernel(
    tc, a, u, r_words, r_scales, v, b_words, b_scales, x, out_0, out_1, out_2
):
    nc = tc.nc
    words_out = out_1[0].rearrange("p m t -> p (m t)")

    with ExitStack() as ctx:
        keep = ctx.enter_context(tc.tile_pool(name="keep", bufs=1))
        work = ctx.enter_context(tc.tile_pool(name="work", bufs=2))
        psum = ctx.enter_context(tc.psum_pool(name="psum", bufs=2))
        ctx.enter_context(tc.manual_schedule())

        rs_raw = keep.tile([128, D], U8, name="rs_raw", align_bytes=64)
        bs = keep.tile([128, P], U8, name="bs", align_bytes=64)
        nc.vector.memset(rs_raw[:].bitcast(I32), 0)
        nc.vector.memset(bs[:].bitcast(I32), 0)
        uv_rows = keep.tile([128, D], BF16, name="uv_rows")
        nc.vector.memset(uv_rows[:].bitcast(I32), 0)
        ident = keep.tile([128, 128], F32, name="ident")
        make_identity(nc, ident[:])

        a_sb = []
        rw_raw = keep.tile([128, 2 * D], U8, name="rw_raw", align_bytes=64)
        for j in range(PAIRS):
            a_j = keep.tile([128, 2, D], BF16, name="a%d" % j)
            nc.sync.dma_start(out=a_j[:], in_=a[256 * j : 256 * j + 256, :].rearrange("(i p) k -> p i k", p=128))
            a_sb.append(a_j)
            if j == 0:
                nc.sync.dma_start(out=rw_raw[:].bitcast(I32), in_=r_words[0].bitcast(I32))
        bw = keep.tile([128, 2 * P], U8, name="bw", align_bytes=64)
        nc.scalar.dma_start(out=uv_rows[0:L, :], in_=u)
        nc.scalar.dma_start(out=uv_rows[L : 2 * L, :], in_=v)
        for q in range(4):
            nc.scalar.dma_start(
                out=rs_raw[32 * q : 32 * q + 4, :].bitcast(I32), in_=r_scales[0, 4 * q : 4 * q + 4, :].bitcast(I32)
            )
        warm = keep.tile([128, 1], F32, name="warm")
        nc.vector.memset(warm[:], 0.0)
        nc.scalar.activation(out=warm[:], in_=warm[:], func=ACTF.Sigmoid)
        nc.sync.dma_start(out=bw[:].bitcast(I32), in_=b_words[0].bitcast(I32))
        for q in range(4):
            nc.sync.dma_start(
                out=bs[32 * q : 32 * q + 4, :].bitcast(I32), in_=b_scales[0, 4 * q : 4 * q + 4, :].bitcast(I32)
            )
        x_sb = []
        for l in range(L):
            x_l = keep.tile([128, TILES, P], BF16, name="x%d" % l)
            x_sb.append(x_l)

        def load_x(l):
            nc.scalar.dma_start(out=x_sb[l][:], in_=x[l].rearrange("(i p) k -> p i k", p=128))

        rw = keep.tile([128, 4, 256], U8, name="rw", align_bytes=64)
        rs = keep.tile([128, 4, 128], U8, name="rs", align_bytes=64)

        def permute_r_words():
            nc.vector.tensor_copy(
                out=rw[:].rearrange("p t (m b) -> p t m b", b=2),
                in_=rw_raw[:].rearrange("p (m t b) -> p t m b", t=4, b=2),
            )

        def permute_r_scales():
            nc.vector.tensor_copy(out=rs[:], in_=rs_raw[:].rearrange("p (m t) -> p t m", t=4))

        uv = keep.tile([128, 2 * L, 4], BF16, name="uv")

        def transpose_uv():
            ps = psum.tile([128, 2, 128], F32, name="ps_uv", tag="s1")
            words = uv_rows[:].bitcast(F32)
            for k in range(2):
                nc.tensor.transpose(ps[:, k, :], words[:, k : 256 : 2], ident[:])
            nc.vector.tensor_copy(out=uv[:].bitcast(F32), in_=ps[:, :, 0 : 2 * L].rearrange("p k r -> p r k"))

        aT = []
        for h in range(2):
            aT_h = keep.tile([128, 512, 4], BF16, name="aT%d" % h, align_bytes=64)
            aT.append(aT_h)

        def transpose_a(j):
            ps = psum.tile([128, 2, 2, 128], F32, name="ps_a", tag="o")
            words = a_sb[j][:].bitcast(F32)
            for i in range(2):
                for k in range(2):
                    nc.tensor.transpose(ps[:, i, k, :], words[:, i, k : 256 : 2], ident[:])
            c0 = 256 * (j % 2)
            dst = aT[j // 2][:, c0 : c0 + 256, :].bitcast(F32).rearrange("p (i n) k -> p i n k", i=2)
            src = ps[:].rearrange("p i k n -> p i n k")
            nc.scalar.copy(out=dst, in_=src)

        def transpose_a_tile(j, i):
            ps = psum.tile([128, 2, 128], F32, name="ps_a1", tag="o")
            words = a_sb[j][:].bitcast(F32)
            for k in range(2):
                nc.tensor.transpose(ps[:, k, :], words[:, i, k : 256 : 2], ident[:])
            c0 = 256 * (j % 2) + 128 * i
            nc.scalar.copy(
                out=aT[j // 2][:, c0 : c0 + 128, :].bitcast(F32), in_=ps[:].rearrange("p k n -> p n k")
            )

        st = {}

        def scale_a(l, h, c0=0, w=512):
            if c0 == 0:
                auq = work.tile([128, 512, 4], BF16, name="auq", bufs=4, align_bytes=64)
                st["auq", l, h] = auq
            cols = slice(c0, c0 + w)
            nc.vector.tensor_tensor(
                out=st["auq", l, h][:, cols, :],
                in0=aT[h][:, cols, :],
                in1=uv[:, l, :].unsqueeze(1).to_broadcast([128, w, 4]),
                op=ALU.mult,
            )

        def make_diagonals(l):
            diag = keep.tile([128, 4, 128], BF16, name="diag%d" % l)
            for t in range(4):
                nc.gpsimd.tensor_scalar(
                    out=diag[:, t, :],
                    in0=ident[:],
                    scalar1=uv[:, l, t : t + 1],
                    scalar2=0.0,
                    op0=ALU.mult,
                    op1=ALU.add,
                )
            st["diag", l] = diag

        def scale_a_chunk(l, c):
            if c % 4 == 0:
                auq = work.tile([128, 512, 4], BF16, name="auq", bufs=4, align_bytes=64)
                st["auq", l, c // 4] = auq
            st["chunk", l, c] = True
            n0 = 128 * (c % 4)
            ps = psum.tile([128, 4, 128], F32, name="ps_u", tag="o" if c % 2 else "s2")
            for t in range(4):
                nc.tensor.matmul(
                    ps[:, t, :],
                    lhsT=st["diag", l][:, t, :],
                    rhs=aT[c // 4][:, n0 : n0 + 128, t],
                    start=True,
                    stop=True,
                )
            nc.scalar.copy(out=st["auq", l, c // 4][:, n0 : n0 + 128, :], in_=ps[:].rearrange("p t n -> p n t"))

        def quant_a(l, h, c0=0, w=512):
            if c0 == 0:
                c = work.tile([128, 512], U32, name="au_c", bufs=2, align_bytes=64)
                s = work.tile([128, 512], U8, name="au_s", bufs=2, align_bytes=64)
                st["au", l, h] = (c, s)
            if l in AU_ACT:
                assert all(("chunk", l, 4 * h + k) in st for k in range(4))
            c, s = st["au", l, h]
            cols = slice(c0, c0 + w)
            nc.vector.quantize_mx(
                out=c[:, cols].bitcast(FP8),
                scales=s[:, cols],
                in_=st["auq", l, h][:, cols, :].rearrange("p n t -> p (n t)"),
            )

        def matmul_1(l, i):
            c, s = st["au", l, i // 4]
            n0 = 128 * (i % 4)
            ps = psum.tile([128, 4, 128], F32, name="ps_t", tag="t")
            for t in range(4):
                nc.tensor.matmul_mx(
                    out=ps[:, t, :],
                    lhsT=rw[:, t, :].bitcast(FP4),
                    lhsT_scale=rs[:, t, :],
                    rhs=c[:, n0 : n0 + 128].bitcast(FP8),
                    rhs_scale=s[:, n0 : n0 + 128],
                    start=True,
                    stop=True,
                )
            st["t", l, i] = ps

        def scale_t(l, i):
            if i % 4 == 0:
                tvq = work.tile([128, 512, 4], BF16, name="tvq", bufs=2, align_bytes=64)
                st["tvq", l, i // 4] = tvq
            n0 = 128 * (i % 4)
            nc.vector.tensor_tensor(
                out=st["tvq", l, i // 4][:, n0 : n0 + 128, :],
                in0=st["t", l, i][:].rearrange("p t n -> p n t"),
                in1=uv[:, L + l, :].unsqueeze(1).to_broadcast([128, 128, 4]),
                op=ALU.mult,
            )

        def quant_t(l, first, count):
            h = first // 4
            if first % 4 == 0:
                c = work.tile([128, 512], U32, name="tv_c", bufs=6, align_bytes=64)
                s = work.tile([128, 512], U8, name="tv_s", bufs=6, align_bytes=64)
                st["tv", l, h] = (c, s)
            c, s = st["tv", l, h]
            cols = slice(128 * (first % 4), 128 * (first % 4 + count))
            nc.vector.quantize_mx(
                out=c[:, cols].bitcast(FP8),
                scales=s[:, cols],
                in_=st["tvq", l, h][:, cols, :].rearrange("p n t -> p (n t)"),
            )

        def matmul_2(l, i, tag, times=1):
            c, s = st["tv", l, i // 4]
            n0 = 128 * (i % 4)
            ps = psum.tile([128, P], F32, name="ps_" + tag, tag=tag)
            for k in range(times):
                nc.tensor.matmul_mx(
                    out=ps[:],
                    lhsT=c[:, n0 : n0 + 128].bitcast(FP8),
                    lhsT_scale=s[:, n0 : n0 + 128],
                    rhs=bw[:].bitcast(FP4),
                    rhs_scale=bs[:],
                    start=True,
                    stop=True,
                )
            return ps

        def sigmoid(l, i):
            ps = matmul_2(l, i, "s1")
            if i % 4 == 0:
                sg = work.tile([128, 4, P], F32, name="sg", bufs=7)
                st["sg", l, i // 4] = sg
            nc.scalar.activation(out=st["sg", l, i // 4][:, i % 4, :], in_=ps[:], func=ACTF.Sigmoid, scale=-1.0)

            st["sig", l, i] = True

        def log(l, first, count=4):
            sg = st["sg", l, first // 4][:, first % 4 : first % 4 + count, :]
            assert all(("sig", l, k) in st for k in range(first, first + count))
            nc.scalar.activation(out=sg, in_=sg, func=ACTF.Ln, bias=DELTA)
            for k in range(first, first + count):
                st["log", l, k] = True

        def scores(l, i):
            tag = "s2" if l == 0 else ("s2", "s2", "t", "t", "s1", "s1")[(8 * (l - 1) + i) % 6]
            st["s", l, i] = matmul_2(l, i, tag, 2 if l > 0 and WARM else 1)

        def loss_parts(l, i):
            ps = st["s", l, i]
            assert ("log", l, i) in st
            xs = work.tile([128, P], F32, name="xs", bufs=6)
            nc.vector.tensor_tensor(out=xs[:], in0=ps[:], in1=x_sb[l][:, i, :], op=ALU.mult)
            sp = work.tile([128, P], F32, name="sp", bufs=6)
            nc.vector.scalar_tensor_tensor(
                out=sp[:], in0=st["sg", l, i // 4][:, i % 4, :], scalar=-1.0, in1=ps[:], op0=ALU.mult, op1=ALU.max
            )
            st["parts", l, i] = (sp, xs)

        def loss(l, i):
            sp, xs = st["parts", l, i]
            if i % 2 == 0:
                res = work.tile([128, 2, P], F32, name="res", bufs=6)
                st["res", l, i // 2] = res
            res = st["res", l, i // 2]
            engine = nc.vector if i in V_TILES[l] else nc.gpsimd
            engine.tensor_tensor(out=res[:, i % 2, :], in0=sp[:], in1=xs[:], op=ALU.subtract)
            if i % 2 == 1:
                n0 = 128 * (i - 1)
                nc.sync.dma_start(
                    out=out_0[l, n0 : n0 + 256, :].rearrange("(i p) k -> p i k", p=128), in_=res[:]
                )

        def round_out(l, first, count):
            j = first // 2
            if first % 2 == 0:
                rb = work.tile([128, 2, P], BF16, name="rb", bufs=3)
                st["rb", l, j] = rb
            part = slice(first % 2, first % 2 + count)
            nc.scalar.copy(out=st["rb", l, j][:, part, :], in_=st["res", l, j][:, part, :])

        def transpose_out(l, j):
            if j % 2 == 0:
                oq = work.tile([128, 512, 4], BF16, name="oq", bufs=3, align_bytes=64)
                st["oq", l, j // 2] = oq
            ps = psum.tile([128, 2, 2, 128], F32, name="ps_o", tag="o")
            for i in range(2):
                words = st["rb", l, j][:, i, :].bitcast(F32)
                for k in range(2):
                    nc.tensor.transpose(ps[:, i, k, :], words[:, k : 256 : 2], ident[:])
            n0 = 256 * (j % 2)
            nc.scalar.copy(
                out=st["oq", l, j // 2][:, n0 : n0 + 256, :].bitcast(F32).rearrange("p (i n) k -> p i n k", i=2),
                in_=ps[:].rearrange("p i k n -> p i n k"),
            )

        def quant_out(l, first, count):
            h = first // 4
            if first == 0:
                o_s = work.tile([128, N], U8, name="o_s", bufs=2, align_bytes=64)
                st["o_s", l] = o_s
            if first % 4 == 0:
                o_c = work.tile([128, 512], U32, name="o_c", bufs=3, align_bytes=64)
                st["o_c", l, h] = o_c
            o_s = st["o_s", l]
            o_c = st["o_c", l, h]
            c0, w = 128 * (first % 4), 128 * count
            nc.vector.quantize_mx(
                out=o_c[:, c0 : c0 + w].bitcast(FP8),
                scales=o_s[:, 128 * first : 128 * first + w],
                in_=st["oq", l, h][:, c0 : c0 + w, :].rearrange("p n t -> p (n t)"),
            )
            m0 = N * l + 128 * first
            nc.sync.dma_start(
                out=words_out[:, 4 * m0 : 4 * (m0 + w)].bitcast(I32), in_=o_c[:, c0 : c0 + w].bitcast(I32)
            )
            if first + count == TILES:
                for q in range(4):
                    nc.sync.dma_start(
                        out=out_2[0, 4 * q : 4 * q + 4, N * l : N * l + N].bitcast(I32),
                        in_=o_s[32 * q : 32 * q + 4, :].bitcast(I32),
                    )

        clock = [0]
        due = {}
        sigmoids = []
        chunks = [(l, c) for l in AU_ACT for c in range(TILES)]

        def later(steps, fn, *args):
            due.setdefault(clock[0] + steps, []).append((fn, args))

        def tick():
            for fn, args in due.pop(clock[0], []):
                fn(*args)
            clock[0] += 1

        def feed_chunk(n=1):
            for k in range(n):
                if chunks:
                    scale_a_chunk(*chunks.pop(0))

        def feed_sigmoid(n=1):
            for k in range(n):
                if sigmoids:
                    sigmoid(*sigmoids.pop(0))

        def finish_tile(l, i):
            n = R_TILES[l]
            if i % n == n - 1:
                round_out(l, i + 1 - n, n)
            if i % 2 == 1:
                later(LAGS[l][1], finish_pair, l, i // 2)

        def finish_pair(l, j):
            transpose_out(l, j)
            n = Q_TILES[l]
            if (2 * j + 2) % n == 0:
                later(LAGS[l][2], quant_out, l, 2 * j + 2 - n, n)

        def front(l):
            if l not in AU_ACT:
                scale_a(l, 0)
                scale_a(l, 1)
            quant_a(l, 0)
            quant_a(l, 1)

        def slot_a(l, acts, first=0):
            n = T_TILES[l]
            for i in range(first, TILES):
                scale_t(l, i)
                if i + 2 < TILES:
                    matmul_1(l, i + 2)
                if i % n == 0 and i > first:
                    quant_t(l, i - n, n)
                    sigmoids.extend([(l, k) for k in range(i - n, i)])
                acts(i)
                tick()
            quant_t(l, TILES - n, n)
            sigmoids.extend([(l, k) for k in range(TILES - n, TILES)])

        def slot_b(l, acts):
            for i in range(TILES):
                loss_parts(l, i)
                if i + LEAD[l] < TILES:
                    scores(l, i + LEAD[l])
                elif l > 0 and l + 1 < L:
                    scores(l + 1, i + LEAD[l] - TILES)
                acts(i)
                if i not in V_TILES[l]:
                    loss(l, i)
                else:
                    later(D_LAG, loss, l, i)
                later(LAGS[l][0], finish_tile, l, i)
                tick()

        def first_scores(l, count):
            for i in range(count):
                scores(l, i)

        def first_matmuls(l):
            matmul_1(l, 0)
            matmul_1(l, 1)

        if RW_FIRST:
            permute_r_words()
        if HEAD1:
            transpose_a_tile(0, 0)
            transpose_uv()
            transpose_a_tile(0, 1)
        else:
            transpose_a(0)
            transpose_uv()
        for l in AU_ACT:
            make_diagonals(l)
        for j in range(1, PAIRS):
            transpose_a(j)
        for l in range(L):
            load_x(l)
        if HEAD1:
            scale_a(0, 0, 0, 128)
            scale_a(0, 0, 128, 128)
            quant_a(0, 0, 0, 128)
            if not RW_FIRST:
                permute_r_words()
            permute_r_scales()
            quant_a(0, 0, 128, 128)
        else:
            scale_a(0, 0, 0, 256)
            if not RW_FIRST:
                permute_r_words()
            quant_a(0, 0, 0, 256)
            permute_r_scales()
        feed_chunk(C0)
        first_matmuls(0)
        scale_a(0, 0, 256, 256)
        if EARLY_T:
            scale_t(0, 0)
            scale_t(0, 1)
            quant_a(0, 0, 256, 256)
        else:
            quant_a(0, 0, 256, 256)
            feed_chunk(C1)
            scale_t(0, 0)
            scale_t(0, 1)
        matmul_1(0, 2)
        matmul_1(0, 3)
        quant_t(0, 0, 2)
        feed_chunk(C2)
        sigmoid(0, 0)
        sigmoid(0, 1)
        scale_a(0, 1)
        quant_a(0, 1)

        def acts_a0(i):
            feed_chunk()
            feed_sigmoid(S0)

        slot_a(0, acts_a0, 2)
        front(1)
        first_matmuls(1)
        feed_sigmoid(S01)

        def acts_a1(i):
            feed_chunk()
            feed_sigmoid(S1)

        slot_a(1, acts_a1)
        front(2)
        first_matmuls(2)
        feed_sigmoid(S12)

        def acts_a2(i):
            if sigmoids and sigmoids[0][0] < 2:
                feed_sigmoid(2)
            elif i in LOG_A2:
                log(*LOG_A2[i])
            if i == 6:
                first_scores(0, 2)

        slot_a(2, acts_a2)
        front(3)

        def acts_b0(i):
            if i == 0:
                for k in (0, 4):
                    if (1, k) not in LOG_A2.values():
                        log(1, k)
            if i >= S2_FROM:
                feed_sigmoid(S2)
            if i == 6:
                first_matmuls(3)

        slot_b(0, acts_b0)

        def acts_a3(i):
            feed_sigmoid(S3)
            if i == 5:
                first_scores(1, 2)

        slot_a(3, acts_a3)
        for i in range(2, LEAD[1]):
            scores(1, i)
        feed_sigmoid(S31)

        def acts_b1(i):
            feed_sigmoid(2)
            if i in LOG_B1:
                log(*LOG_B1[i])

        def acts_b2(i):
            if i in LOG_B2:
                log(*LOG_B2[i])

        slot_b(1, acts_b1)
        slot_b(2, acts_b2)
        slot_b(3, lambda i: None)
        while due:
            tick()
